import numpy as np
import ml_dtypes


def mxq(x, axis, fmt="e4m3"):
    dtype, down = {"e4m3": (ml_dtypes.float8_e4m3fn, 7), "e5m2": (ml_dtypes.float8_e5m2, 14)}[fmt]
    v = np.moveaxis(np.asarray(x, np.float32).astype(ml_dtypes.bfloat16).astype(np.float64), axis, -1)
    blocks = v.reshape(v.shape[:-1] + (-1, 32))
    amax = np.abs(blocks).max(-1, keepdims=True)
    byte = np.maximum(np.where(amax > 0, np.frexp(amax)[1] - 1 + 127, 0) - down, 1)
    scale = np.exp2(byte - 127.0)
    codes = (blocks / scale).astype(np.float32).astype(dtype).astype(np.float64)
    return np.moveaxis((codes * scale).reshape(v.shape), -1, axis)


WIDE = False


def mx_kscale(k):
    if not WIDE:
        return np.ones(k)
    levels = np.array([10, -10, 5, -5, 0])
    if k % 512:
        return np.exp2(np.random.permutation(np.resize(levels, k // 32))).repeat(32)
    a = np.empty((k // 512, 16))
    for p in range(k // 512):
        a[p, :8] = np.random.permutation(np.resize(levels, 8))
        for g in range(8):
            far = levels[np.abs(levels - a[p, g]) >= 10]
            a[p, g + 8] = far[np.random.randint(len(far))]
    return np.exp2(a.ravel()).repeat(32)


def f64(x):
    return np.asarray(x).astype(np.float64)


def striped(idx):
    return np.tile(idx.reshape(-1, 16).T, (8, 1)).astype(np.uint16)


def unstriped(offs):
    return offs[:16].T.reshape(-1).astype(np.int64)


E2M1 = np.array([0.0, 0.5, 1.0, 1.5, 2.0, 3.0, 4.0, 6.0, -0.0, -0.5, -1.0, -1.5, -2.0, -3.0, -4.0, -6.0])


def pack_weight(w, fmt):
    k, n = w.shape
    w = f64(np.asarray(w, np.float32).astype(ml_dtypes.bfloat16)).reshape(k // 32, 32, n)
    amax = np.abs(w).max(1)
    if fmt == "e4m3":
        byte = np.frexp(amax)[1] - 1 + 127 - 7
    else:
        mant, ex = np.frexp(amax / 6.0)
        byte = np.where(mant > 0.5, ex, ex - 1) + 127
    byte = np.clip(np.where(amax > 0, byte, 1), 1, 254)
    scaled = (w * np.exp2(127.0 - byte)[:, None, :]).reshape(k, n).astype(np.float32)
    by_word = np.ascontiguousarray(scaled.reshape(k // 512, 128, 4, n).transpose(0, 1, 3, 2))
    if fmt == "e4m3":
        words = by_word.astype(ml_dtypes.float8_e4m3fn).view(np.uint8)
    else:
        c = by_word.astype(ml_dtypes.float4_e2m1fn).view(np.uint8) & 0xF
        words = (c[..., 0::2] | (c[..., 1::2] << 4)).reshape(k // 512, 128, 2 * n)
    return np.ascontiguousarray(words), np.ascontiguousarray(byte.astype(np.uint8).reshape(k // 512, 16, n))


def unpack_weight(words, scales, fmt):
    g, _, n = scales.shape
    words = np.ascontiguousarray(words).reshape(g, 128, n, -1)
    if fmt == "e4m3":
        vals = words.view(ml_dtypes.float8_e4m3fn).astype(np.float64)
    else:
        nib = np.empty((g, 128, n, 4), np.uint8)
        nib[..., 0::2] = words & 0xF
        nib[..., 1::2] = words >> 4
        vals = E2M1[nib]
    vals = vals * np.repeat(np.exp2(scales.astype(np.float64) - 127.0), 8, axis=1)[..., None]
    return vals.transpose(0, 1, 3, 2).reshape(g * 512, n)


def gelu(v):
    return 0.5 * v * (1.0 + np.tanh(np.sqrt(2.0 / np.pi) * (v + 0.044715 * v**3)))


K, H, T, S, P = 512, 1024, 4096, 1024, 512


def setup_inputs():
    n = np.random.standard_normal
    s = mx_kscale(K)[:, None]
    u = mx_kscale(H)[:, None]
    tab_words, tab_scales = pack_weight(n((K, T)) * s, "e4m3")
    shared = n((K, H))
    w1 = 0.9 * (shared + n((K, H))) / np.sqrt(K) / s
    w2 = 0.9 * (shared + n((K, H))) / np.sqrt(K) / s
    w3 = 0.9 * (shared + n((K, H))) / np.sqrt(K) / s
    w2_words, w2_scales = pack_weight(w2, "e2m1")
    w3_words, w3_scales = pack_weight(w3, "e4m3")
    gain = np.random.uniform(0.6, 1.6, H) * u[:, 0]
    dv = n(H) / np.sqrt(H) / u[:, 0] ** 2
    base = 0.8 * n((H, P)) * u
    rel = np.exp(0.5 * n((P, P)))
    return {"tab_words": tab_words, "tab_scales": tab_scales,
            "w1": w1.astype(np.float32),
            "w2_words": w2_words, "w2_scales": w2_scales,
            "w3_words": w3_words, "w3_scales": w3_scales,
            "gain": gain.astype(np.float32), "dv": dv.astype(np.float32),
            "base": base.astype(np.float32), "rel": rel.astype(np.float32),
            "offs": striped(np.random.permutation(T)[:S]),
            "pos1": striped(np.random.permutation(S)[:P]),
            "pos2": striped(np.random.permutation(S)[:P])}


def reference(tab_words, tab_scales, w1, w2_words, w2_scales, w3_words, w3_scales,
              gain, dv, base, rel, offs, pos1, pos2):
    v = unpack_weight(tab_words, tab_scales, "e4m3")[:, unstriped(offs)]
    r1 = mxq(f64(w1), 0, "e4m3").T @ v
    r2 = unpack_weight(w2_words, w2_scales, "e2m1").T @ v
    r3 = unpack_weight(w3_words, w3_scales, "e4m3").T @ v
    h = np.tanh(np.maximum(np.maximum(r1, r2), r3)) * f64(gain)[:, None]
    x1 = mxq(h[:, unstriped(pos1)], 0, "e4m3")
    x2 = mxq(np.abs(h[:, unstriped(pos2)]) * f64(dv)[:, None], 0, "e4m3")
    e = x1.T @ x2 + mxq(f64(base), 0, "e4m3").T @ x2
    return e * f64(rel)

@@ -1,0 +1,280 @@
+from contextlib import ExitStack
+
+import concourse.mybir as mybir
+
+K, H, T, S, NP = 512, 1024, 4096, 1024, 512
+FLOPS = 2 * (3 * K * H * S + 2 * H * NP * NP)
+
+F32 = mybir.dt.float32
+BF16 = mybir.dt.bfloat16
+I32 = mybir.dt.int32
+U32 = mybir.dt.uint32
+U16 = mybir.dt.uint16
+U8 = mybir.dt.uint8
+FP8X4 = mybir.dt.float8_e4m3fn_x4
+FP4X4 = mybir.dt.float4_e2m1fn_x4
+ACT = mybir.ActivationFunctionType
+ALU = mybir.AluOpType
+
+P = 128
+PACK = 4
+PASS = P * PACK
+HALF = 512
+NB = H // PASS
+NSLICE = NB * PACK
+MT = NP // P
+
+
+def tile_list_clause_importability_scores_kernel(
+    tc, tab_words, tab_scales, w1, w2_words, w2_scales, w3_words, w3_scales,
+    gain, dv, base, rel, offs, pos1, pos2, out,
+):
+    nc = tc.nc
+    with ExitStack() as ctx:
+        keep = ctx.enter_context(tc.tile_pool(name="keep", bufs=1))
+        stage = ctx.enter_context(tc.tile_pool(name="stage", bufs=2))
+        work = ctx.enter_context(tc.tile_pool(name="work", bufs=2))
+        psum = ctx.enter_context(tc.psum_pool(name="psum", bufs=8))
+
+        offs_t = keep.tile([P, S // 16], U16, name="offs_t")
+        pos1_t = keep.tile([P, NP // 16], U16, name="pos1_t")
+        pos2_t = keep.tile([P, NP // 16], U16, name="pos2_t")
+        tab_w = keep.tile([P, T], I32, name="tab_w", align_bytes=64)
+        tab_s = keep.tile([P, T], U8, name="tab_s", align_bytes=64)
+        w2_raw = keep.tile([P, 2 * H], U8, name="w2_raw", tag="small_b", align_bytes=64)
+        w2s_raw = keep.tile([P, H], U8, name="w2s_raw", tag="small_a", align_bytes=64)
+        w3s_raw = keep.tile([P, H], U8, name="w3s_raw", align_bytes=64)
+
+        nc.vector.memset(tab_s[:].bitcast(I32), 0)
+        nc.gpsimd.memset(w2s_raw[:].bitcast(I32), 0)
+        nc.gpsimd.memset(w3s_raw[:].bitcast(I32), 0)
+
+        def load_scale_rows(queue, tile, rows, quadrant):
+            queue.dma_start(
+                out=tile[:].bitcast(I32)[32 * quadrant : 32 * quadrant + 4, :],
+                in_=rows[0, 4 * quadrant : 4 * quadrant + 4, :].bitcast(I32),
+            )
+
+        w3_view = w3_words[0].rearrange("p c i -> p (c i)").bitcast(I32)
+
+        def load_w3(b):
+            raw = stage.tile([P, PASS], I32, name="w3_raw", tag="stage", align_bytes=64)
+            nc.sync.dma_start(out=raw[:], in_=w3_view[:, PASS * b : PASS * (b + 1)])
+            return raw
+
+        def load_rows(rows):
+            raw = stage.tile([P, PACK, 512], F32, name="raw", tag="stage", align_bytes=64)
+            nc.sync.dma_start(out=raw[:], in_=rows)
+            return raw
+
+        w1_view = w1.rearrange("(p j) r -> p j r", j=PACK)
+        base_view = base.rearrange("(b p t) m -> b p t m", b=NB, t=PACK)
+
+        nc.sync.dma_start(offs_t[:], offs)
+        nc.sync.dma_start(pos1_t[:], pos1)
+        nc.sync.dma_start(pos2_t[:], pos2)
+        nc.sync.dma_start(out=w2_raw[:].bitcast(I32), in_=w2_words[0].bitcast(I32))
+        w3_raw0 = load_w3(0)
+        nc.sync.dma_start(out=tab_w[:], in_=tab_words[0].rearrange("p t i -> p (t i)").bitcast(I32))
+        w1_raw0 = load_rows(w1_view[:, :, 0:PASS])
+        for q in range(4):
+            load_scale_rows(nc.scalar, tab_s, tab_scales, q)
+        for q in range(4):
+            load_scale_rows(nc.scalar if q < 2 else nc.gpsimd, w2s_raw, w2_scales, q)
+        for q in range(4):
+            load_scale_rows(nc.gpsimd, w3s_raw, w3_scales, q)
+
+        w2_p = keep.tile([P, 2 * H], U8, name="w2_p", align_bytes=64)
+        w2s_p = keep.tile([P, H], U8, name="w2s_p", align_bytes=64)
+        w3s_p = keep.tile([P, H], U8, name="w3s_p", align_bytes=64)
+        w3_p = [keep.tile([P, PASS], I32, name="w3_p%d" % b, align_bytes=64) for b in range(NB)]
+
+        def deal_w3(raw, b):
+            nc.vector.tensor_copy(
+                out=w3_p[b][:].rearrange("p (t q) -> p q t", t=PACK),
+                in_=raw[:].rearrange("p (q t) -> p q t", t=PACK),
+            )
+
+        nc.vector.tensor_copy(
+            out=w2_p[:].rearrange("p (b t q e) -> p b t q e", b=NB, t=PACK, e=2),
+            in_=w2_raw[:].rearrange("p (b q t e) -> p b t q e", b=NB, t=PACK, e=2),
+        )
+        deal_w3(w3_raw0, 0)
+        v_s = keep.tile([P, S], U8, name="v_s", align_bytes=64)
+        nc.vector.tensor_copy(v_s[:], tab_s[:].indirect(offs_t[:]))
+
+        def deal_scales(dealt, raw, b0, b1):
+            nc.vector.tensor_copy(
+                out=dealt[:].rearrange("p (b t q) -> p b t q", b=NB, t=PACK)[:, b0:b1],
+                in_=raw[:].rearrange("p (b q t) -> p b t q", b=NB, t=PACK)[:, b0:b1],
+            )
+
+        deal_scales(w2s_p, w2s_raw, 0, NB)
+        gain_t = keep.tile([P, NB, PACK], F32, name="gain_t", tag="small_a", align_bytes=64)
+        dv_t = keep.tile([P, NB, PACK], F32, name="dv_t", tag="small_b", align_bytes=64)
+        nc.sync.dma_start(out=gain_t[:], in_=gain.rearrange("(b p t) -> p b t", b=NB, t=PACK))
+        nc.sync.dma_start(out=dv_t[:], in_=dv.rearrange("(b p t) -> p b t", b=NB, t=PACK))
+        v_w = [keep.tile([P, HALF], U32, name="v_w%d" % h, align_bytes=64) for h in range(2)]
+        for h in range(2):
+            nc.vector.tensor_copy(v_w[h][:], tab_w[:].bitcast(U32).indirect(offs_t[:, 32 * h : 32 * (h + 1)]))
+            if h == 0:
+                deal_scales(w3s_p, w3s_raw, 0, 1)
+
+        w1_i = [keep.tile([P, PACK, P, PACK], BF16, name="w1_i%d" % b, align_bytes=64) for b in range(NB)]
+        w1_c = [keep.tile([P, PASS], U32, name="w1_c%d" % b, align_bytes=64) for b in range(NB)]
+        w1_s = [keep.tile([P, PASS], U8, name="w1_s%d" % b, align_bytes=64) for b in range(NB)]
+
+        def round_w1(raw, b, t0, t1, q0, q1):
+            nc.scalar.activation(
+                out=w1_i[b][:].rearrange("p t q j -> p q j t")[:, q0:q1, :, t0:t1],
+                in_=raw[:].rearrange("p j (q t) -> p q j t", t=PACK)[:, q0:q1, :, t0:t1],
+                func=ACT.Copy,
+            )
+
+        def quantize_w1(b, t0, t1):
+            nc.vector.quantize_mx(
+                out=w1_c[b][:, P * t0 : P * t1].bitcast(FP8X4),
+                scales=w1_s[b][:, P * t0 : P * t1],
+                in_=w1_i[b][:, t0:t1].rearrange("p t q j -> p (t q j)"),
+            )
+
+        def operand(name):
+            woven = [keep.tile([P, NP, PACK], BF16, name="%s_i%d" % (name, b), align_bytes=64) for b in range(NB)]
+            codes = [keep.tile([P, NP], U32, name="%s_c%d" % (name, b), align_bytes=64) for b in range(NB)]
+            scales = [keep.tile([P, NP], U8, name="%s_s%d" % (name, b), align_bytes=64) for b in range(NB)]
+            return woven, codes, scales
+
+        x1_op, x2_op, base_op = operand("x1"), operand("x2"), operand("base")
+
+        def weave(op, b, planes, c0, c1, slots=PACK):
+            nc.scalar.activation(
+                out=op[0][b][:, c0:c1, 0:slots].rearrange("p (c i) t -> p c t i", i=4),
+                in_=planes[:, 0:slots, c0:c1].rearrange("p t (c i) -> p c t i", i=4),
+                func=ACT.Copy,
+            )
+
+        def quantize(op, b, c0=0, c1=NP):
+            nc.vector.quantize_mx(
+                out=op[1][b][:, c0:c1].bitcast(FP8X4),
+                scales=op[2][b][:, c0:c1],
+                in_=op[0][b][:, c0:c1, :].rearrange("p c t -> p (c t)"),
+            )
+
+        x1_planes = [keep.tile([P, PACK, NP], F32, name="x1_pl%d" % b) for b in range(NB)]
+        x2_planes = [keep.tile([P, PACK, NP], F32, name="x2_pl%d" % b) for b in range(NB)]
+
+        def first_stage(s):
+            b, t = divmod(s, PACK)
+            cols = slice(P * s, P * (s + 1))
+            in_pass = slice(P * t, P * (t + 1))
+            sides = (
+                (w2_p[:, 2 * P * s : 2 * P * (s + 1)].bitcast(FP4X4), w2s_p[:, cols]),
+                (w3_p[b][:, in_pass].bitcast(FP8X4), w3s_p[:, cols]),
+                (w1_c[b][:, in_pass].bitcast(FP8X4), w1_s[b][:, in_pass]),
+            )
+            banks = []
+            for codes, scales in sides:
+                for h in range(2):
+                    bank = psum.tile([P, HALF], F32, name="bank", tag="bank")
+                    nc.tensor.matmul_mx(
+                        out=bank[:], lhsT=codes, lhsT_scale=scales,
+                        rhs=v_w[h][:].bitcast(FP8X4), rhs_scale=v_s[:, HALF * h : HALF * (h + 1)],
+                        start=True, stop=True,
+                    )
+                    banks.append(bank)
+            r2 = [work.tile([P, HALF], F32, name="r2_%d" % h, bufs=3) for h in range(2)]
+            m23 = [work.tile([P, HALF], F32, name="m23_%d" % h) for h in range(2)]
+            top = work.tile([P, S], F32, name="top")
+            bent = work.tile([P, S], F32, name="bent", bufs=3)
+            for h in range(2):
+                nc.scalar.activation(out=r2[h][:], in_=banks[h][:], func=ACT.Copy)
+            for h in range(2):
+                nc.vector.tensor_tensor(m23[h][:], banks[2 + h][:], r2[h][:], ALU.max)
+            for h in range(2):
+                nc.vector.tensor_tensor(top[:, HALF * h : HALF * (h + 1)], banks[4 + h][:], m23[h][:], ALU.max)
+            if s == NSLICE - 1:
+                for h in range(2):
+                    part = slice(HALF * h, HALF * (h + 1))
+                    nc.scalar.activation(out=bent[:, part], in_=top[:, part], func=ACT.Tanh)
+            else:
+                nc.scalar.activation(out=bent[:], in_=top[:], func=ACT.Tanh)
+            return bent
+
+        def pick(s, bent):
+            b, t = divmod(s, PACK)
+            g2 = work.tile([P, NP], F32, name="g2")
+            g1 = work.tile([P, NP], F32, name="g1")
+            a2 = work.tile([P, NP], F32, name="a2")
+            nc.vector.tensor_copy(g2[:], bent[:].indirect(pos2_t[:]))
+            nc.vector.tensor_copy(g1[:], bent[:].indirect(pos1_t[:]))
+            nc.scalar.activation(out=a2[:], in_=g2[:], func=ACT.Abs, scale=gain_t[:, b, t : t + 1])
+            if s == NSLICE - 1:
+                nc.scalar.activation(out=x2_op[0][b][:, :, t], in_=a2[:], func=ACT.Copy, scale=dv_t[:, b, t : t + 1])
+            else:
+                nc.vector.tensor_scalar(x2_planes[b][:, t, :], a2[:], dv_t[:, b, t : t + 1], None, ALU.mult)
+            if s >= NSLICE - 2:
+                nc.vector.tensor_scalar(x1_op[0][b][:, :, t], g1[:], gain_t[:, b, t : t + 1], None, ALU.mult)
+            else:
+                nc.vector.tensor_scalar(x1_planes[b][:, t, :], g1[:], gain_t[:, b, t : t + 1], None, ALU.mult)
+
+        round_w1(w1_raw0, 0, 0, 1, 0, P)
+        quantize_w1(0, 0, 1)
+        bent = first_stage(0)
+        round_w1(w1_raw0, 0, 1, PACK, 0, P)
+        quantize_w1(0, 1, PACK)
+        deal_w3(load_w3(1), 1)
+        deal_scales(w3s_p, w3s_raw, 1, NB)
+        staged = {}
+        for s in range(1, NSLICE):
+            nxt = first_stage(s)
+            pick(s - 1, bent)
+            bent = nxt
+            if s == 1:
+                staged["w1"] = load_rows(w1_view[:, :, PASS : 2 * PASS])
+                round_w1(staged["w1"], 1, 0, PACK, 0, P // 2)
+            if s == 2:
+                round_w1(staged["w1"], 1, 0, PACK, P // 2, P)
+                quantize_w1(1, 0, PACK)
+                staged["base0"] = load_rows(base_view[0])
+                weave(base_op, 0, staged["base0"], 0, 256)
+            if s == 3:
+                weave(base_op, 0, staged["base0"], 256, 512)
+                quantize(base_op, 0)
+                staged["base1"] = load_rows(base_view[1])
+                weave(base_op, 1, staged["base1"], 0, 256)
+            if s == 4:
+                weave(base_op, 1, staged["base1"], 256, 512)
+                quantize(base_op, 1)
+                staged["rel"] = load_rows(rel.rearrange("(a p) j -> p a j", p=P))
+                weave(x2_op, 0, x2_planes[0], 0, 256)
+            if s == 5:
+                weave(x2_op, 0, x2_planes[0], 256, 512)
+                quantize(x2_op, 0)
+                weave(x1_op, 0, x1_planes[0], 0, 256)
+            if s == 6:
+                weave(x1_op, 0, x1_planes[0], 256, 512)
+                quantize(x1_op, 0)
+            if s == 7:
+                weave(x1_op, 1, x1_planes[1], 0, 512, 2)
+                weave(x2_op, 1, x2_planes[1], 0, 512, 3)
+        pick(NSLICE - 1, bent)
+        quantize(x2_op, 1)
+        for a in range(MT):
+            quantize(x1_op, 1, P * a, P * (a + 1))
+
+        sums = [psum.tile([P, NP], F32, name="bank", tag="bank") for a in range(MT)]
+        passes = ((x1_op, 0), (base_op, 0), (base_op, 1), (x1_op, 1))
+        for first, last in ((0, 2), (2, 3), (3, 4)):
+            for a in range(MT):
+                cols = slice(P * a, P * (a + 1))
+                for n in range(first, last):
+                    op, b = passes[n]
+                    nc.tensor.matmul_mx(
+                        out=sums[a][:], lhsT=op[1][b][:, cols].bitcast(FP8X4), lhsT_scale=op[2][b][:, cols],
+                        rhs=x2_op[1][b][:].bitcast(FP8X4), rhs_scale=x2_op[2][b][:],
+                        start=(n == 0), stop=(n == len(passes) - 1),
+                    )
+        for a in range(MT):
+            res = work.tile([P, NP], F32, name="res", bufs=4)
+            nc.vector.tensor_tensor(res[:], sums[a][:], staged["rel"][:, a, :], ALU.mult)
+            nc.sync.dma_start(out=out[P * a : P * (a + 1), :], in_=res[:])

@@ -32,22 +32,19 @@ def tile_list_clause_importability_scores_kernel(
     nc = tc.nc
     with ExitStack() as ctx:
         keep = ctx.enter_context(tc.tile_pool(name="keep", bufs=1))
-        stage = ctx.enter_context(tc.tile_pool(name="stage", bufs=2))
         work = ctx.enter_context(tc.tile_pool(name="work", bufs=2))
         psum = ctx.enter_context(tc.psum_pool(name="psum", bufs=8))
 
         offs_t = keep.tile([P, S // 16], U16, name="offs_t")
         pos1_t = keep.tile([P, NP // 16], U16, name="pos1_t")
         pos2_t = keep.tile([P, NP // 16], U16, name="pos2_t")
-        tab_w = keep.tile([P, T], I32, name="tab_w", align_bytes=64)
-        tab_s = keep.tile([P, T], U8, name="tab_s", align_bytes=64)
-        w2_raw = keep.tile([P, 2 * H], U8, name="w2_raw", tag="small_b", align_bytes=64)
-        w2s_raw = keep.tile([P, H], U8, name="w2s_raw", tag="small_a", align_bytes=64)
-        w3s_raw = keep.tile([P, H], U8, name="w3s_raw", align_bytes=64)
+        tab_w = keep.tile([P, T], I32, name="tab_w", tag="lane_b", align_bytes=64)
+        tab_s = keep.tile([P, T], U8, name="tab_s", tag="lane_c", align_bytes=64)
+        w2_raw = keep.tile([P, 2 * H], U8, name="w2_raw", tag="lane_a", align_bytes=64)
+        ws_raw = keep.tile([P, H], U8, name="ws_raw", tag="lane_d", align_bytes=64)
 
         nc.vector.memset(tab_s[:].bitcast(I32), 0)
-        nc.gpsimd.memset(w2s_raw[:].bitcast(I32), 0)
-        nc.gpsimd.memset(w3s_raw[:].bitcast(I32), 0)
+        nc.gpsimd.memset(ws_raw[:].bitcast(I32), 0)
 
         def load_scale_rows(queue, tile, rows, quadrant):
             queue.dma_start(
@@ -57,13 +54,13 @@ def tile_list_clause_importability_scores_kernel(
 
         w3_view = w3_words[0].rearrange("p c i -> p (c i)").bitcast(I32)
 
-        def load_w3(b):
-            raw = stage.tile([P, PASS], I32, name="w3_raw", tag="stage", align_bytes=64)
+        def load_w3(b, lane):
+            raw = keep.tile([P, PASS], I32, name="w3_raw", tag=lane, align_bytes=64)
             nc.sync.dma_start(out=raw[:], in_=w3_view[:, PASS * b : PASS * (b + 1)])
             return raw
 
-        def load_rows(rows):
-            raw = stage.tile([P, PACK, 512], F32, name="raw", tag="stage", align_bytes=64)
+        def load_rows(rows, lane):
+            raw = keep.tile([P, PACK, 512], F32, name="raw", tag=lane, align_bytes=64)
             nc.sync.dma_start(out=raw[:], in_=rows)
             return raw
 
@@ -74,15 +71,11 @@ def tile_list_clause_importability_scores_kernel(
         nc.sync.dma_start(pos1_t[:], pos1)
         nc.sync.dma_start(pos2_t[:], pos2)
         nc.sync.dma_start(out=w2_raw[:].bitcast(I32), in_=w2_words[0].bitcast(I32))
-        w3_raw0 = load_w3(0)
         nc.sync.dma_start(out=tab_w[:], in_=tab_words[0].rearrange("p t i -> p (t i)").bitcast(I32))
-        w1_raw0 = load_rows(w1_view[:, :, 0:PASS])
         for q in range(4):
             load_scale_rows(nc.scalar, tab_s, tab_scales, q)
         for q in range(4):
-            load_scale_rows(nc.scalar if q < 2 else nc.gpsimd, w2s_raw, w2_scales, q)
-        for q in range(4):
-            load_scale_rows(nc.gpsimd, w3s_raw, w3_scales, q)
+            load_scale_rows(nc.scalar if q < 2 else nc.gpsimd, ws_raw, w2_scales, q)
 
         w2_p = keep.tile([P, 2 * H], U8, name="w2_p", align_bytes=64)
         w2s_p = keep.tile([P, H], U8, name="w2s_p", align_bytes=64)
@@ -95,30 +88,26 @@ def tile_list_clause_importability_scores_kernel(
                 in_=raw[:].rearrange("p (q t) -> p q t", t=PACK),
             )
 
+        def deal_scales(dealt):
+            nc.vector.tensor_copy(
+                out=dealt[:].rearrange("p (b t q) -> p b t q", b=NB, t=PACK),
+                in_=ws_raw[:].rearrange("p (b q t) -> p b t q", b=NB, t=PACK),
+            )
+
         nc.vector.tensor_copy(
             out=w2_p[:].rearrange("p (b t q e) -> p b t q e", b=NB, t=PACK, e=2),
             in_=w2_raw[:].rearrange("p (b q t e) -> p b t q e", b=NB, t=PACK, e=2),
         )
-        deal_w3(w3_raw0, 0)
+        w1_raw0 = load_rows(w1_view[:, :, 0:PASS], "lane_a")
         v_s = keep.tile([P, S], U8, name="v_s", align_bytes=64)
         nc.vector.tensor_copy(v_s[:], tab_s[:].indirect(offs_t[:]))
-
-        def deal_scales(dealt, raw, b0, b1):
-            nc.vector.tensor_copy(
-                out=dealt[:].rearrange("p (b t q) -> p b t q", b=NB, t=PACK)[:, b0:b1],
-                in_=raw[:].rearrange("p (b q t) -> p b t q", b=NB, t=PACK)[:, b0:b1],
-            )
-
-        deal_scales(w2s_p, w2s_raw, 0, NB)
-        gain_t = keep.tile([P, NB, PACK], F32, name="gain_t", tag="small_a", align_bytes=64)
-        dv_t = keep.tile([P, NB, PACK], F32, name="dv_t", tag="small_b", align_bytes=64)
-        nc.sync.dma_start(out=gain_t[:], in_=gain.rearrange("(b p t) -> p b t", b=NB, t=PACK))
-        nc.sync.dma_start(out=dv_t[:], in_=dv.rearrange("(b p t) -> p b t", b=NB, t=PACK))
+        w3_raw0 = load_w3(0, "lane_c")
+        deal_scales(w2s_p)
+        for q in range(4):
+            load_scale_rows(nc.sync, ws_raw, w3_scales, q)
         v_w = [keep.tile([P, HALF], U32, name="v_w%d" % h, align_bytes=64) for h in range(2)]
         for h in range(2):
             nc.vector.tensor_copy(v_w[h][:], tab_w[:].bitcast(U32).indirect(offs_t[:, 32 * h : 32 * (h + 1)]))
-            if h == 0:
-                deal_scales(w3s_p, w3s_raw, 0, 1)
 
         w1_i = [keep.tile([P, PACK, P, PACK], BF16, name="w1_i%d" % b, align_bytes=64) for b in range(NB)]
         w1_c = [keep.tile([P, PASS], U32, name="w1_c%d" % b, align_bytes=64) for b in range(NB)]
@@ -160,38 +149,48 @@ def tile_list_clause_importability_scores_kernel(
                 in_=op[0][b][:, c0:c1, :].rearrange("p c t -> p (c t)"),
             )
 
+        def weave_base(b, planes, c0, c1):
+            nc.gpsimd.tensor_scalar(
+                base_op[0][b][:, c0:c1, :], planes[:, :, c0:c1].rearrange("p t c -> p c t"), 1.0, 0.0, ALU.mult, ALU.add
+            )
+
         x1_planes = [keep.tile([P, PACK, NP], F32, name="x1_pl%d" % b) for b in range(NB)]
         x2_planes = [keep.tile([P, PACK, NP], F32, name="x2_pl%d" % b) for b in range(NB)]
 
-        def first_stage(s):
-            b, t = divmod(s, PACK)
-            cols = slice(P * s, P * (s + 1))
-            in_pass = slice(P * t, P * (t + 1))
-            sides = (
-                (w2_p[:, 2 * P * s : 2 * P * (s + 1)].bitcast(FP4X4), w2s_p[:, cols]),
-                (w3_p[b][:, in_pass].bitcast(FP8X4), w3s_p[:, cols]),
-                (w1_c[b][:, in_pass].bitcast(FP8X4), w1_s[b][:, in_pass]),
-            )
+        def product(codes, scales):
             banks = []
-            for codes, scales in sides:
-                for h in range(2):
-                    bank = psum.tile([P, HALF], F32, name="bank", tag="bank")
-                    nc.tensor.matmul_mx(
-                        out=bank[:], lhsT=codes, lhsT_scale=scales,
-                        rhs=v_w[h][:].bitcast(FP8X4), rhs_scale=v_s[:, HALF * h : HALF * (h + 1)],
-                        start=True, stop=True,
-                    )
-                    banks.append(bank)
+            for h in range(2):
+                bank = psum.tile([P, HALF], F32, name="bank", tag="bank")
+                nc.tensor.matmul_mx(
+                    out=bank[:], lhsT=codes, lhsT_scale=scales,
+                    rhs=v_w[h][:].bitcast(FP8X4), rhs_scale=v_s[:, HALF * h : HALF * (h + 1)],
+                    start=True, stop=True,
+                )
+                banks.append(bank)
+            return banks
+
+        def second_reading(s):
+            banks = product(w2_p[:, 2 * P * s : 2 * P * (s + 1)].bitcast(FP4X4), w2s_p[:, P * s : P * (s + 1)])
             r2 = [work.tile([P, HALF], F32, name="r2_%d" % h, bufs=3) for h in range(2)]
-            m23 = [work.tile([P, HALF], F32, name="m23_%d" % h) for h in range(2)]
-            top = work.tile([P, S], F32, name="top")
-            bent = work.tile([P, S], F32, name="bent", bufs=3)
             for h in range(2):
                 nc.scalar.activation(out=r2[h][:], in_=banks[h][:], func=ACT.Copy)
+            return r2
+
+        def strongest(s, r2):
+            b, t = divmod(s, PACK)
+            in_pass = slice(P * t, P * (t + 1))
+            r1 = product(w1_c[b][:, in_pass].bitcast(FP8X4), w1_s[b][:, in_pass])
+            r3 = product(w3_p[b][:, in_pass].bitcast(FP8X4), w3s_p[:, P * s : P * (s + 1)])
+            m12 = [keep.tile([P, HALF], F32, name="m12", tag="turn_%d_%d" % (s % 2, h)) for h in range(2)]
+            top = work.tile([P, S], F32, name="top")
             for h in range(2):
-                nc.vector.tensor_tensor(m23[h][:], banks[2 + h][:], r2[h][:], ALU.max)
+                nc.vector.tensor_tensor(m12[h][:], r1[h][:], r2[h][:], ALU.max)
             for h in range(2):
-                nc.vector.tensor_tensor(top[:, HALF * h : HALF * (h + 1)], banks[4 + h][:], m23[h][:], ALU.max)
+                nc.vector.tensor_tensor(top[:, HALF * h : HALF * (h + 1)], r3[h][:], m12[h][:], ALU.max)
+            return top
+
+        def bend(s, top):
+            bent = work.tile([P, S], F32, name="bent", bufs=3)
             if s == NSLICE - 1:
                 for h in range(2):
                     part = slice(HALF * h, HALF * (h + 1))
@@ -202,8 +201,8 @@ def tile_list_clause_importability_scores_kernel(
 
         def pick(s, bent):
             b, t = divmod(s, PACK)
-            g2 = work.tile([P, NP], F32, name="g2")
-            g1 = work.tile([P, NP], F32, name="g1")
+            g2 = keep.tile([P, NP], F32, name="g2", tag="turn_%d_0" % ((s + 1) % 2))
+            g1 = keep.tile([P, NP], F32, name="g1", tag="turn_%d_1" % ((s + 1) % 2))
             a2 = work.tile([P, NP], F32, name="a2")
             nc.vector.tensor_copy(g2[:], bent[:].indirect(pos2_t[:]))
             nc.vector.tensor_copy(g1[:], bent[:].indirect(pos1_t[:]))
@@ -211,41 +210,55 @@ def tile_list_clause_importability_scores_kernel(
             if s == NSLICE - 1:
                 nc.scalar.activation(out=x2_op[0][b][:, :, t], in_=a2[:], func=ACT.Copy, scale=dv_t[:, b, t : t + 1])
             else:
-                nc.vector.tensor_scalar(x2_planes[b][:, t, :], a2[:], dv_t[:, b, t : t + 1], None, ALU.mult)
+                nc.gpsimd.tensor_scalar(x2_planes[b][:, t, :], a2[:], dv_t[:, b, t : t + 1], 0.0, ALU.mult, ALU.add)
             if s >= NSLICE - 2:
                 nc.vector.tensor_scalar(x1_op[0][b][:, :, t], g1[:], gain_t[:, b, t : t + 1], None, ALU.mult)
             else:
-                nc.vector.tensor_scalar(x1_planes[b][:, t, :], g1[:], gain_t[:, b, t : t + 1], None, ALU.mult)
+                nc.gpsimd.tensor_scalar(x1_planes[b][:, t, :], g1[:], gain_t[:, b, t : t + 1], 0.0, ALU.mult, ALU.add)
 
-        round_w1(w1_raw0, 0, 0, 1, 0, P)
-        quantize_w1(0, 0, 1)
-        bent = first_stage(0)
-        round_w1(w1_raw0, 0, 1, PACK, 0, P)
-        quantize_w1(0, 1, PACK)
-        deal_w3(load_w3(1), 1)
-        deal_scales(w3s_p, w3s_raw, 1, NB)
+        r2_now = second_reading(0)
+        nc.vector.tensor_copy(
+            out=w1_i[0][:].rearrange("p t q j -> p q j t")[:, :, :, 0:2],
+            in_=w1_raw0[:].rearrange("p j (q t) -> p q j t", t=PACK)[:, :, :, 0:2],
+        )
+        deal_w3(w3_raw0, 0)
+        quantize_w1(0, 0, 2)
+        deal_scales(w3s_p)
+        gain_t = keep.tile([P, NB, PACK], F32, name="gain_t", tag="lane_d", align_bytes=64)
+        dv_t = keep.tile([P, NB, PACK], F32, name="dv_t", tag="lane_c", align_bytes=64)
+        nc.sync.dma_start(out=dv_t[:], in_=dv.rearrange("(b p t) -> p b t", b=NB, t=PACK))
+        nc.sync.dma_start(out=gain_t[:], in_=gain.rearrange("(b p t) -> p b t", b=NB, t=PACK))
+        top = strongest(0, r2_now)
+        r2_now = second_reading(1)
+        bent = bend(0, top)
+        round_w1(w1_raw0, 0, 2, PACK, 0, P)
+        quantize_w1(0, 2, PACK)
+        deal_w3(load_w3(1, "lane_a"), 1)
         staged = {}
         for s in range(1, NSLICE):
-            nxt = first_stage(s)
+            top = strongest(s, r2_now)
+            if s + 1 < NSLICE:
+                r2_now = second_reading(s + 1)
+            nxt = bend(s, top)
             pick(s - 1, bent)
             bent = nxt
             if s == 1:
-                staged["w1"] = load_rows(w1_view[:, :, PASS : 2 * PASS])
+                staged["w1"] = load_rows(w1_view[:, :, PASS : 2 * PASS], "lane_a")
                 round_w1(staged["w1"], 1, 0, PACK, 0, P // 2)
             if s == 2:
                 round_w1(staged["w1"], 1, 0, PACK, P // 2, P)
                 quantize_w1(1, 0, PACK)
-                staged["base0"] = load_rows(base_view[0])
-                weave(base_op, 0, staged["base0"], 0, 256)
+                staged["base0"] = load_rows(base_view[0], "lane_b")
+                weave_base(0, staged["base0"], 0, 256)
             if s == 3:
-                weave(base_op, 0, staged["base0"], 256, 512)
+                weave_base(0, staged["base0"], 256, 512)
                 quantize(base_op, 0)
-                staged["base1"] = load_rows(base_view[1])
-                weave(base_op, 1, staged["base1"], 0, 256)
+                staged["base1"] = load_rows(base_view[1], "lane_b")
+                weave_base(1, staged["base1"], 0, 256)
             if s == 4:
-                weave(base_op, 1, staged["base1"], 256, 512)
+                weave_base(1, staged["base1"], 256, 512)
                 quantize(base_op, 1)
-                staged["rel"] = load_rows(rel.rearrange("(a p) j -> p a j", p=P))
+                staged["rel"] = load_rows(rel.rearrange("(a p) j -> p a j", p=P), "lane_a")
                 weave(x2_op, 0, x2_planes[0], 0, 256)
             if s == 5:
                 weave(x2_op, 0, x2_planes[0], 256, 512)
@@ -264,7 +277,7 @@ def tile_list_clause_importability_scores_kernel(
 
         sums = [psum.tile([P, NP], F32, name="bank", tag="bank") for a in range(MT)]
         passes = ((x1_op, 0), (base_op, 0), (base_op, 1), (x1_op, 1))
-        for first, last in ((0, 2), (2, 3), (3, 4)):
+        for first, last in ((0, 2), (2, 4)):
             for a in range(MT):
                 cols = slice(P * a, P * (a + 1))
                 for n in range(first, last):

@@ -77,6 +77,24 @@ def tile_list_clause_importability_scores_kernel(
         for q in range(4):
             load_scale_rows(nc.scalar if q < 2 else nc.gpsimd, ws_raw, w2_scales, q)
 
+        gain_t = keep.tile([P, NB, PACK], F32, name="gain_t")
+        dv_t = keep.tile([P, NB, PACK], F32, name="dv_t")
+        nc.gpsimd.dma_start(out=gain_t[:], in_=gain.rearrange("(b p t) -> p b t", b=NB, t=PACK))
+        nc.gpsimd.dma_start(out=dv_t[:], in_=dv.rearrange("(b p t) -> p b t", b=NB, t=PACK))
+        f1 = [keep.tile([P, NP], F32, name="f1_%d" % s) for s in range(NSLICE)]
+        f2 = [keep.tile([P, NP], F32, name="f2_%d" % s) for s in range(NSLICE)]
+        sign_t = keep.tile([P, NB, PACK], BF16, name="sign_t")
+
+        def spread_factors(s):
+            b, t = divmod(s, PACK)
+            row_gain = gain_t[:, b, t : t + 1].to_broadcast([P, NP])
+            nc.scalar.activation(out=f2[s][:], in_=row_gain, func=ACT.Copy, scale=dv_t[:, b, t : t + 1])
+            nc.scalar.activation(out=f1[s][:], in_=row_gain, func=ACT.Copy)
+
+        nc.scalar.activation(out=sign_t[:], in_=dv_t[:], func=ACT.Sign)
+        for s in range(PACK):
+            spread_factors(s)
+
         w2_p = keep.tile([P, 2 * H], U8, name="w2_p", align_bytes=64)
         w2s_p = keep.tile([P, H], U8, name="w2s_p", align_bytes=64)
         w3s_p = keep.tile([P, H], U8, name="w3s_p", align_bytes=64)
@@ -135,11 +153,11 @@ def tile_list_clause_importability_scores_kernel(
 
         x1_op, x2_op, base_op = operand("x1"), operand("x2"), operand("base")
 
-        def weave(op, b, planes, c0, c1, slots=PACK):
+        def weave(op, b, planes, c0, c1, slots=PACK, func=ACT.Copy):
             nc.scalar.activation(
                 out=op[0][b][:, c0:c1, 0:slots].rearrange("p (c i) t -> p c t i", i=4),
                 in_=planes[:, 0:slots, c0:c1].rearrange("p t (c i) -> p c t i", i=4),
-                func=ACT.Copy,
+                func=func,
             )
 
         def quantize(op, b, c0=0, c1=NP):
@@ -150,9 +168,7 @@ def tile_list_clause_importability_scores_kernel(
             )
 
         def weave_base(b, planes, c0, c1):
-            nc.gpsimd.tensor_scalar(
-                base_op[0][b][:, c0:c1, :], planes[:, :, c0:c1].rearrange("p t c -> p c t"), 1.0, 0.0, ALU.mult, ALU.add
-            )
+            weave(base_op, b, planes, c0, c1)
 
         x1_planes = [keep.tile([P, PACK, NP], F32, name="x1_pl%d" % b) for b in range(NB)]
         x2_planes = [keep.tile([P, PACK, NP], F32, name="x2_pl%d" % b) for b in range(NB)]
@@ -181,12 +197,13 @@ def tile_list_clause_importability_scores_kernel(
             in_pass = slice(P * t, P * (t + 1))
             r1 = product(w1_c[b][:, in_pass].bitcast(FP8X4), w1_s[b][:, in_pass])
             r3 = product(w3_p[b][:, in_pass].bitcast(FP8X4), w3s_p[:, P * s : P * (s + 1)])
-            m12 = [keep.tile([P, HALF], F32, name="m12", tag="turn_%d_%d" % (s % 2, h)) for h in range(2)]
+            pb, pt = divmod((s - 1) % NSLICE, PACK)
+            m12 = [x2_planes[pb][:, pt, :], x1_planes[pb][:, pt, :]]
             top = work.tile([P, S], F32, name="top")
             for h in range(2):
-                nc.vector.tensor_tensor(m12[h][:], r1[h][:], r2[h][:], ALU.max)
+                nc.vector.tensor_tensor(m12[h], r1[h][:], r2[h][:], ALU.max)
             for h in range(2):
-                nc.vector.tensor_tensor(top[:, HALF * h : HALF * (h + 1)], r3[h][:], m12[h][:], ALU.max)
+                nc.vector.tensor_tensor(top[:, HALF * h : HALF * (h + 1)], r3[h][:], m12[h], ALU.max)
             return top
 
         def bend(s, top):
@@ -201,33 +218,20 @@ def tile_list_clause_importability_scores_kernel(
 
         def pick(s, bent):
             b, t = divmod(s, PACK)
-            g2 = keep.tile([P, NP], F32, name="g2", tag="turn_%d_0" % ((s + 1) % 2))
-            g1 = keep.tile([P, NP], F32, name="g1", tag="turn_%d_1" % ((s + 1) % 2))
-            a2 = work.tile([P, NP], F32, name="a2")
-            nc.vector.tensor_copy(g2[:], bent[:].indirect(pos2_t[:]))
-            nc.vector.tensor_copy(g1[:], bent[:].indirect(pos1_t[:]))
-            nc.scalar.activation(out=a2[:], in_=g2[:], func=ACT.Abs, scale=gain_t[:, b, t : t + 1])
-            if s == NSLICE - 1:
-                nc.scalar.activation(out=x2_op[0][b][:, :, t], in_=a2[:], func=ACT.Copy, scale=dv_t[:, b, t : t + 1])
-            else:
-                nc.gpsimd.tensor_scalar(x2_planes[b][:, t, :], a2[:], dv_t[:, b, t : t + 1], 0.0, ALU.mult, ALU.add)
-            if s >= NSLICE - 2:
-                nc.vector.tensor_scalar(x1_op[0][b][:, :, t], g1[:], gain_t[:, b, t : t + 1], None, ALU.mult)
-            else:
-                nc.gpsimd.tensor_scalar(x1_planes[b][:, t, :], g1[:], gain_t[:, b, t : t + 1], 0.0, ALU.mult, ALU.add)
+            nc.vector.tensor_tensor(x2_planes[b][:, t, :], bent[:].indirect(pos2_t[:]), f2[s][:], ALU.mult)
+            nc.vector.tensor_tensor(x1_planes[b][:, t, :], bent[:].indirect(pos1_t[:]), f1[s][:], ALU.mult)
+
+        def restore_sign(b, c0, c1):
+            woven = x2_op[0][b][:, c0:c1, :]
+            nc.vector.tensor_tensor(
+                woven, woven, sign_t[:, b : b + 1, :].to_broadcast([P, c1 - c0, PACK]), ALU.mult
+            )
 
         r2_now = second_reading(0)
-        nc.vector.tensor_copy(
-            out=w1_i[0][:].rearrange("p t q j -> p q j t")[:, :, :, 0:2],
-            in_=w1_raw0[:].rearrange("p j (q t) -> p q j t", t=PACK)[:, :, :, 0:2],
-        )
+        round_w1(w1_raw0, 0, 0, 2, 0, P)
         deal_w3(w3_raw0, 0)
         quantize_w1(0, 0, 2)
         deal_scales(w3s_p)
-        gain_t = keep.tile([P, NB, PACK], F32, name="gain_t", tag="lane_d", align_bytes=64)
-        dv_t = keep.tile([P, NB, PACK], F32, name="dv_t", tag="lane_c", align_bytes=64)
-        nc.sync.dma_start(out=dv_t[:], in_=dv.rearrange("(b p t) -> p b t", b=NB, t=PACK))
-        nc.sync.dma_start(out=gain_t[:], in_=gain.rearrange("(b p t) -> p b t", b=NB, t=PACK))
         top = strongest(0, r2_now)
         r2_now = second_reading(1)
         bent = bend(0, top)
@@ -259,21 +263,30 @@ def tile_list_clause_importability_scores_kernel(
                 weave_base(1, staged["base1"], 256, 512)
                 quantize(base_op, 1)
                 staged["rel"] = load_rows(rel.rearrange("(a p) j -> p a j", p=P), "lane_a")
-                weave(x2_op, 0, x2_planes[0], 0, 256)
+                weave(x2_op, 0, x2_planes[0], 0, 256, PACK, ACT.Abs)
             if s == 5:
-                weave(x2_op, 0, x2_planes[0], 256, 512)
-                quantize(x2_op, 0)
+                weave(x2_op, 0, x2_planes[0], 256, 512, PACK, ACT.Abs)
+                restore_sign(0, 0, NP)
                 weave(x1_op, 0, x1_planes[0], 0, 256)
             if s == 6:
+                quantize(x2_op, 0)
                 weave(x1_op, 0, x1_planes[0], 256, 512)
                 quantize(x1_op, 0)
             if s == 7:
-                weave(x1_op, 1, x1_planes[1], 0, 512, 2)
-                weave(x2_op, 1, x2_planes[1], 0, 512, 3)
+                weave(x2_op, 1, x2_planes[1], 0, 512, 3, ACT.Abs)
+                weave(x1_op, 1, x1_planes[1], 0, 512, 3)
+            if 2 <= s < 2 + PACK:
+                spread_factors(s + 2)
         pick(NSLICE - 1, bent)
+        for h in range(2):
+            cols = slice(256 * h, 256 * (h + 1))
+            nc.scalar.activation(out=x2_op[0][1][:, cols, 3], in_=x2_planes[1][:, 3, cols], func=ACT.Abs)
+            restore_sign(1, cols.start, cols.stop)
         quantize(x2_op, 1)
         for a in range(MT):
-            quantize(x1_op, 1, P * a, P * (a + 1))
+            cols = slice(P * a, P * (a + 1))
+            nc.scalar.activation(out=x1_op[0][1][:, cols, 3], in_=x1_planes[1][:, 3, cols], func=ACT.Copy)
+            quantize(x1_op, 1, cols.start, cols.stop)
 
         sums = [psum.tile([P, NP], F32, name="bank", tag="bank") for a in range(MT)]
         passes = ((x1_op, 0), (base_op, 0), (base_op, 1), (x1_op, 1))

@@ -32,19 +32,23 @@ def tile_list_clause_importability_scores_kernel(
     nc = tc.nc
     with ExitStack() as ctx:
         keep = ctx.enter_context(tc.tile_pool(name="keep", bufs=1))
+        after_tab = ctx.enter_context(tc.tile_pool(name="after_tab", bufs=1))
+        after_w2 = ctx.enter_context(tc.tile_pool(name="after_w2", bufs=1))
         work = ctx.enter_context(tc.tile_pool(name="work", bufs=2))
         psum = ctx.enter_context(tc.psum_pool(name="psum", bufs=8))
 
         offs_t = keep.tile([P, S // 16], U16, name="offs_t")
         pos1_t = keep.tile([P, NP // 16], U16, name="pos1_t")
         pos2_t = keep.tile([P, NP // 16], U16, name="pos2_t")
-        tab_w = keep.tile([P, T], I32, name="tab_w", tag="lane_b", align_bytes=64)
+        tab_w = after_tab.tile([P, T], I32, name="tab_w", align_bytes=64, offset=0)
         tab_s = keep.tile([P, T], U8, name="tab_s", tag="lane_c", align_bytes=64)
-        w2_raw = keep.tile([P, 2 * H], U8, name="w2_raw", tag="lane_a", align_bytes=64)
-        ws_raw = keep.tile([P, H], U8, name="ws_raw", tag="lane_d", align_bytes=64)
+        w2_raw = after_w2.tile([P, 2 * H], U8, name="w2_raw", align_bytes=64, offset=1536)
+        w2s_raw = keep.tile([P, H], U8, name="w2s_raw", align_bytes=64)
+        gain_t = keep.tile([P, NB, PACK], F32, name="gain_t")
+        dv_t = keep.tile([P, NB, PACK], F32, name="dv_t")
 
         nc.vector.memset(tab_s[:].bitcast(I32), 0)
-        nc.gpsimd.memset(ws_raw[:].bitcast(I32), 0)
+        nc.gpsimd.memset(w2s_raw[:].bitcast(I32), 0)
 
         def load_scale_rows(queue, tile, rows, quadrant):
             queue.dma_start(
@@ -54,14 +58,19 @@ def tile_list_clause_importability_scores_kernel(
 
         w3_view = w3_words[0].rearrange("p c i -> p (c i)").bitcast(I32)
 
-        def load_w3(b, lane):
-            raw = keep.tile([P, PASS], I32, name="w3_raw", tag=lane, align_bytes=64)
+        def load_w3(b):
+            raw = after_w2.tile([P, PASS], I32, name="w3_raw", align_bytes=64, offset=0)
             nc.sync.dma_start(out=raw[:], in_=w3_view[:, PASS * b : PASS * (b + 1)])
             return raw
 
-        def load_rows(rows, lane):
-            raw = keep.tile([P, PACK, 512], F32, name="raw", tag=lane, align_bytes=64)
+        def load_rows(rows):
+            raw = after_w2.tile([P, PACK, 512], F32, name="raw", align_bytes=64, offset=3072)
             nc.sync.dma_start(out=raw[:], in_=rows)
+            return raw
+
+        def load_base(b):
+            raw = after_tab.tile([P, PACK, NP], F32, name="base_raw", align_bytes=64, offset=8192)
+            nc.sync.dma_start(out=raw[:], in_=base_view[b])
             return raw
 
         w1_view = w1.rearrange("(p j) r -> p j r", j=PACK)
@@ -75,66 +84,61 @@ def tile_list_clause_importability_scores_kernel(
         for q in range(4):
             load_scale_rows(nc.scalar, tab_s, tab_scales, q)
         for q in range(4):
-            load_scale_rows(nc.scalar if q < 2 else nc.gpsimd, ws_raw, w2_scales, q)
-
-        gain_t = keep.tile([P, NB, PACK], F32, name="gain_t")
-        dv_t = keep.tile([P, NB, PACK], F32, name="dv_t")
+            load_scale_rows(nc.scalar if q < 2 else nc.gpsimd, w2s_raw, w2_scales, q)
         nc.gpsimd.dma_start(out=gain_t[:], in_=gain.rearrange("(b p t) -> p b t", b=NB, t=PACK))
         nc.gpsimd.dma_start(out=dv_t[:], in_=dv.rearrange("(b p t) -> p b t", b=NB, t=PACK))
-        f1 = [keep.tile([P, NP], F32, name="f1_%d" % s) for s in range(NSLICE)]
-        f2 = [keep.tile([P, NP], F32, name="f2_%d" % s) for s in range(NSLICE)]
-        sign_t = keep.tile([P, NB, PACK], BF16, name="sign_t")
 
-        def spread_factors(s):
+        f1 = [keep.tile([P, NP], F32, name="f1", tag="f1_%d" % s, align_bytes=64) for s in range(NSLICE)]
+        for s in range(NSLICE):
             b, t = divmod(s, PACK)
-            row_gain = gain_t[:, b, t : t + 1].to_broadcast([P, NP])
-            nc.scalar.activation(out=f2[s][:], in_=row_gain, func=ACT.Copy, scale=dv_t[:, b, t : t + 1])
-            nc.scalar.activation(out=f1[s][:], in_=row_gain, func=ACT.Copy)
-
-        nc.scalar.activation(out=sign_t[:], in_=dv_t[:], func=ACT.Sign)
-        for s in range(PACK):
-            spread_factors(s)
+            nc.scalar.activation(out=f1[s][:], in_=gain_t[:, b, t : t + 1].to_broadcast([P, NP]), func=ACT.Copy)
 
         w2_p = keep.tile([P, 2 * H], U8, name="w2_p", align_bytes=64)
-        w2s_p = keep.tile([P, H], U8, name="w2s_p", align_bytes=64)
-        w3s_p = keep.tile([P, H], U8, name="w3s_p", align_bytes=64)
-        w3_p = [keep.tile([P, PASS], I32, name="w3_p%d" % b, align_bytes=64) for b in range(NB)]
+        w3_p = {}
 
-        def deal_w3(raw, b):
+        def deal_w3(raw, b, dealt):
+            w3_p[b] = dealt
             nc.vector.tensor_copy(
-                out=w3_p[b][:].rearrange("p (t q) -> p q t", t=PACK),
+                out=dealt[:].rearrange("p (t q) -> p q t", t=PACK),
                 in_=raw[:].rearrange("p (q t) -> p q t", t=PACK),
             )
 
-        def deal_scales(dealt):
+        def deal_scales(dealt, raw):
             nc.vector.tensor_copy(
                 out=dealt[:].rearrange("p (b t q) -> p b t q", b=NB, t=PACK),
-                in_=ws_raw[:].rearrange("p (b q t) -> p b t q", b=NB, t=PACK),
+                in_=raw[:].rearrange("p (b q t) -> p b t q", b=NB, t=PACK),
             )
 
         nc.vector.tensor_copy(
             out=w2_p[:].rearrange("p (b t q e) -> p b t q e", b=NB, t=PACK, e=2),
             in_=w2_raw[:].rearrange("p (b q t e) -> p b t q e", b=NB, t=PACK, e=2),
         )
-        w1_raw0 = load_rows(w1_view[:, :, 0:PASS], "lane_a")
+        w1_raw0 = load_rows(w1_view[:, :, 0:PASS])
+        w3_raw0 = load_w3(0)
+        w3s_raw = after_w2.tile([P, H], U8, name="w3s_raw", align_bytes=64, offset=2048)
+        nc.gpsimd.memset(w3s_raw[:].bitcast(I32), 0)
+        for q in range(4):
+            load_scale_rows(nc.sync, w3s_raw, w3_scales, q)
         v_s = keep.tile([P, S], U8, name="v_s", align_bytes=64)
         nc.vector.tensor_copy(v_s[:], tab_s[:].indirect(offs_t[:]))
-        w3_raw0 = load_w3(0, "lane_c")
-        deal_scales(w2s_p)
-        for q in range(4):
-            load_scale_rows(nc.sync, ws_raw, w3_scales, q)
+        w2s_p = keep.tile([P, H], U8, name="w2s_p", tag="lane_c", align_bytes=64)
+        deal_scales(w2s_p, w2s_raw)
         v_w = [keep.tile([P, HALF], U32, name="v_w%d" % h, align_bytes=64) for h in range(2)]
         for h in range(2):
             nc.vector.tensor_copy(v_w[h][:], tab_w[:].bitcast(U32).indirect(offs_t[:, 32 * h : 32 * (h + 1)]))
 
-        w1_i = [keep.tile([P, PACK, P, PACK], BF16, name="w1_i%d" % b, align_bytes=64) for b in range(NB)]
-        w1_c = [keep.tile([P, PASS], U32, name="w1_c%d" % b, align_bytes=64) for b in range(NB)]
+        w1_i = {
+            (0, 0): keep.tile([P, 2, P, PACK], BF16, name="w1_i00", align_bytes=64),
+            (0, 2): keep.tile([P, 2, P, PACK], BF16, name="w1_i02", align_bytes=64),
+            (1, 0): keep.tile([P, PACK, P, PACK], BF16, name="w1_i10", align_bytes=64),
+        }
+        w1_c = {0: after_tab.tile([P, PASS], U32, name="w1_c0", align_bytes=64, offset=0)}
         w1_s = [keep.tile([P, PASS], U8, name="w1_s%d" % b, align_bytes=64) for b in range(NB)]
 
         def round_w1(raw, b, t0, t1, q0, q1):
             nc.scalar.activation(
-                out=w1_i[b][:].rearrange("p t q j -> p q j t")[:, q0:q1, :, t0:t1],
-                in_=raw[:].rearrange("p j (q t) -> p q j t", t=PACK)[:, q0:q1, :, t0:t1],
+                out=w1_i[b, t0][:].rearrange("p t q j -> p q t j")[:, q0:q1],
+                in_=raw[:].rearrange("p j (q t) -> p q t j", t=PACK)[:, q0:q1, t0:t1, :],
                 func=ACT.Copy,
             )
 
@@ -142,23 +146,34 @@ def tile_list_clause_importability_scores_kernel(
             nc.vector.quantize_mx(
                 out=w1_c[b][:, P * t0 : P * t1].bitcast(FP8X4),
                 scales=w1_s[b][:, P * t0 : P * t1],
-                in_=w1_i[b][:, t0:t1].rearrange("p t q j -> p (t q j)"),
+                in_=w1_i[b, t0][:].rearrange("p t q j -> p (t q j)"),
             )
 
         def operand(name):
-            woven = [keep.tile([P, NP, PACK], BF16, name="%s_i%d" % (name, b), align_bytes=64) for b in range(NB)]
-            codes = [keep.tile([P, NP], U32, name="%s_c%d" % (name, b), align_bytes=64) for b in range(NB)]
+            woven = {}
+            codes = {}
             scales = [keep.tile([P, NP], U8, name="%s_s%d" % (name, b), align_bytes=64) for b in range(NB)]
             return woven, codes, scales
 
         x1_op, x2_op, base_op = operand("x1"), operand("x2"), operand("base")
 
-        def weave(op, b, planes, c0, c1, slots=PACK, func=ACT.Copy):
+        def weave(op, b, planes, c0, c1, slots=PACK):
             nc.scalar.activation(
                 out=op[0][b][:, c0:c1, 0:slots].rearrange("p (c i) t -> p c t i", i=4),
                 in_=planes[:, 0:slots, c0:c1].rearrange("p t (c i) -> p c t i", i=4),
-                func=func,
+                func=ACT.Copy,
             )
+
+        def place_woven(op, b, tag):
+            op[0][b] = keep.tile([P, NP, PACK], BF16, name="woven", tag=tag, align_bytes=64)
+
+        for b in range(NB):
+            place_woven(x1_op, b, "x1_i%d" % b)
+
+        place_woven(x2_op, 0, "x2_i0")
+
+        def place_codes(op, b, tag):
+            op[1][b] = keep.tile([P, NP], U32, name="codes", tag=tag, align_bytes=64)
 
         def quantize(op, b, c0=0, c1=NP):
             nc.vector.quantize_mx(
@@ -187,7 +202,10 @@ def tile_list_clause_importability_scores_kernel(
 
         def second_reading(s):
             banks = product(w2_p[:, 2 * P * s : 2 * P * (s + 1)].bitcast(FP4X4), w2s_p[:, P * s : P * (s + 1)])
-            r2 = [work.tile([P, HALF], F32, name="r2_%d" % h, bufs=3) for h in range(2)]
+            if s == 0:
+                r2 = [after_w2.tile([P, HALF], F32, name="r2_first%d" % h, align_bytes=64, offset=3072 + 2048 * h) for h in range(2)]
+            else:
+                r2 = [work.tile([P, HALF], F32, name="r2_%d" % h, bufs=3) for h in range(2)]
             for h in range(2):
                 nc.scalar.activation(out=r2[h][:], in_=banks[h][:], func=ACT.Copy)
             return r2
@@ -197,9 +215,14 @@ def tile_list_clause_importability_scores_kernel(
             in_pass = slice(P * t, P * (t + 1))
             r1 = product(w1_c[b][:, in_pass].bitcast(FP8X4), w1_s[b][:, in_pass])
             r3 = product(w3_p[b][:, in_pass].bitcast(FP8X4), w3s_p[:, P * s : P * (s + 1)])
-            pb, pt = divmod((s - 1) % NSLICE, PACK)
-            m12 = [x2_planes[pb][:, pt, :], x1_planes[pb][:, pt, :]]
-            top = work.tile([P, S], F32, name="top")
+            last = s == NSLICE - 1
+            pb, pt = divmod(s if last else (s - 1) % NSLICE, PACK)
+            tag = "f1_%d" % (s - 1) if last else "turn_%d" % (s % 2)
+            m12 = [keep.tile([P, HALF], F32, name="m12", tag=tag, align_bytes=64)[:], x1_planes[pb][:, pt, :]]
+            if last:
+                top = keep.tile([P, S], F32, name="top_last", tag="x2_i1", align_bytes=64)
+            else:
+                top = work.tile([P, S], F32, name="top")
             for h in range(2):
                 nc.vector.tensor_tensor(m12[h], r1[h][:], r2[h][:], ALU.max)
             for h in range(2):
@@ -218,79 +241,86 @@ def tile_list_clause_importability_scores_kernel(
 
         def pick(s, bent):
             b, t = divmod(s, PACK)
-            nc.vector.tensor_tensor(x2_planes[b][:, t, :], bent[:].indirect(pos2_t[:]), f2[s][:], ALU.mult)
+            g2 = keep.tile([P, NP], F32, name="g2", tag="turn_%d" % ((s + 1) % 2), align_bytes=64)
+            a2 = work.tile([P, NP], F32, name="a2")
+            nc.vector.tensor_copy(g2[:], bent[:].indirect(pos2_t[:]))
             nc.vector.tensor_tensor(x1_planes[b][:, t, :], bent[:].indirect(pos1_t[:]), f1[s][:], ALU.mult)
+            nc.scalar.activation(out=a2[:], in_=g2[:], func=ACT.Abs, scale=gain_t[:, b, t : t + 1])
+            if s == NSLICE - 1:
+                nc.scalar.activation(out=x2_op[0][b][:, :, t], in_=a2[:], func=ACT.Copy, scale=dv_t[:, b, t : t + 1])
+            else:
+                nc.gpsimd.tensor_scalar(x2_planes[b][:, t, :], a2[:], dv_t[:, b, t : t + 1], 0.0, ALU.mult, ALU.add)
 
-        def restore_sign(b, c0, c1):
-            woven = x2_op[0][b][:, c0:c1, :]
-            nc.vector.tensor_tensor(
-                woven, woven, sign_t[:, b : b + 1, :].to_broadcast([P, c1 - c0, PACK]), ALU.mult
-            )
-
-        r2_now = second_reading(0)
         round_w1(w1_raw0, 0, 0, 2, 0, P)
-        deal_w3(w3_raw0, 0)
+        round_w1(w1_raw0, 0, 2, PACK, 0, P)
+        r2_now = second_reading(0)
         quantize_w1(0, 0, 2)
-        deal_scales(w3s_p)
+        deal_w3(w3_raw0, 0, after_tab.tile([P, PASS], I32, name="w3_p0", align_bytes=64, offset=2048))
+        w3s_p = after_tab.tile([P, H], U8, name="w3s_p", align_bytes=64, offset=4096)
+        deal_scales(w3s_p, w3s_raw)
+        quantize_w1(0, 2, PACK)
         top = strongest(0, r2_now)
         r2_now = second_reading(1)
         bent = bend(0, top)
-        round_w1(w1_raw0, 0, 2, PACK, 0, P)
-        quantize_w1(0, 2, PACK)
-        deal_w3(load_w3(1, "lane_a"), 1)
+        w3_raw1 = load_w3(1)
         staged = {}
-        for s in range(1, NSLICE):
+        for s in range(1, NSLICE - 1):
             top = strongest(s, r2_now)
-            if s + 1 < NSLICE:
-                r2_now = second_reading(s + 1)
+            r2_now = second_reading(s + 1)
             nxt = bend(s, top)
             pick(s - 1, bent)
             bent = nxt
             if s == 1:
-                staged["w1"] = load_rows(w1_view[:, :, PASS : 2 * PASS], "lane_a")
+                deal_w3(w3_raw1, 1, keep.tile([P, PASS], I32, name="w3_p1", tag="f1_0", align_bytes=64))
+                staged["w1"] = load_rows(w1_view[:, :, PASS : 2 * PASS])
                 round_w1(staged["w1"], 1, 0, PACK, 0, P // 2)
             if s == 2:
                 round_w1(staged["w1"], 1, 0, PACK, P // 2, P)
+                w1_c[1] = keep.tile([P, PASS], U32, name="w1_c1", tag="f1_1", align_bytes=64)
                 quantize_w1(1, 0, PACK)
-                staged["base0"] = load_rows(base_view[0], "lane_b")
-                weave_base(0, staged["base0"], 0, 256)
+                staged["base0"] = load_rows(base_view[0])
+                staged["base1"] = load_base(1)
             if s == 3:
-                weave_base(0, staged["base0"], 256, 512)
-                quantize(base_op, 0)
-                staged["base1"] = load_rows(base_view[1], "lane_b")
+                place_woven(base_op, 1, "f1_2")
                 weave_base(1, staged["base1"], 0, 256)
-            if s == 4:
                 weave_base(1, staged["base1"], 256, 512)
-                quantize(base_op, 1)
-                staged["rel"] = load_rows(rel.rearrange("(a p) j -> p a j", p=P), "lane_a")
-                weave(x2_op, 0, x2_planes[0], 0, 256, PACK, ACT.Abs)
+                place_woven(base_op, 0, "base_i0")
+                weave_base(0, staged["base0"], 0, 256)
+            if s == 4:
+                weave_base(0, staged["base0"], 256, 512)
+                place_codes(base_op, 0, "f1_3")
+                quantize(base_op, 0)
+                staged["rel"] = load_rows(rel.rearrange("(a p) j -> p a j", p=P))
+                weave(x2_op, 0, x2_planes[0], 0, 256)
             if s == 5:
-                weave(x2_op, 0, x2_planes[0], 256, 512, PACK, ACT.Abs)
-                restore_sign(0, 0, NP)
+                weave(x2_op, 0, x2_planes[0], 256, 512)
+                place_codes(x2_op, 0, "x2_c0")
+                quantize(x2_op, 0)
                 weave(x1_op, 0, x1_planes[0], 0, 256)
             if s == 6:
-                quantize(x2_op, 0)
                 weave(x1_op, 0, x1_planes[0], 256, 512)
-                quantize(x1_op, 0)
-            if s == 7:
-                weave(x2_op, 1, x2_planes[1], 0, 512, 3, ACT.Abs)
-                weave(x1_op, 1, x1_planes[1], 0, 512, 3)
-            if 2 <= s < 2 + PACK:
-                spread_factors(s + 2)
+        pick(NSLICE - 2, bent)
+        top = strongest(NSLICE - 1, r2_now)
+        bent = bend(NSLICE - 1, top)
+        weave(x1_op, 1, x1_planes[1], 0, 512, 3)
+        place_woven(x2_op, 1, "x2_i1")
+        weave(x2_op, 1, x2_planes[1], 0, 512, 3)
+        place_codes(base_op, 1, "f1_6")
+        quantize(base_op, 1)
         pick(NSLICE - 1, bent)
-        for h in range(2):
-            cols = slice(256 * h, 256 * (h + 1))
-            nc.scalar.activation(out=x2_op[0][1][:, cols, 3], in_=x2_planes[1][:, 3, cols], func=ACT.Abs)
-            restore_sign(1, cols.start, cols.stop)
+        place_codes(x1_op, 0, "f1_7")
+        quantize(x1_op, 0)
+        place_codes(x2_op, 1, "x2_c1")
         quantize(x2_op, 1)
+        place_codes(x1_op, 1, "x1_c1")
         for a in range(MT):
             cols = slice(P * a, P * (a + 1))
             nc.scalar.activation(out=x1_op[0][1][:, cols, 3], in_=x1_planes[1][:, 3, cols], func=ACT.Copy)
             quantize(x1_op, 1, cols.start, cols.stop)
 
         sums = [psum.tile([P, NP], F32, name="bank", tag="bank") for a in range(MT)]
-        passes = ((x1_op, 0), (base_op, 0), (base_op, 1), (x1_op, 1))
-        for first, last in ((0, 2), (2, 4)):
+        passes = ((base_op, 0), (x1_op, 0), (base_op, 1), (x1_op, 1))
+        for first, last in ((0, 1), (1, 2), (2, 4)):
             for a in range(MT):
                 cols = slice(P * a, P * (a + 1))
                 for n in range(first, last):

@@ -43,9 +43,8 @@ def tile_list_clause_importability_scores_kernel(
         tab_w = after_tab.tile([P, T], I32, name="tab_w", align_bytes=64, offset=0)
         tab_s = keep.tile([P, T], U8, name="tab_s", tag="lane_c", align_bytes=64)
         w2_raw = after_w2.tile([P, 2 * H], U8, name="w2_raw", align_bytes=64, offset=1536)
-        w2s_raw = keep.tile([P, H], U8, name="w2s_raw", align_bytes=64)
+        w2s_raw = keep.tile([P, H], U8, name="w2s_raw", tag="lane_d", align_bytes=64)
         gain_t = keep.tile([P, NB, PACK], F32, name="gain_t")
-        dv_t = keep.tile([P, NB, PACK], F32, name="dv_t")
 
         nc.vector.memset(tab_s[:].bitcast(I32), 0)
         nc.gpsimd.memset(w2s_raw[:].bitcast(I32), 0)
@@ -85,8 +84,8 @@ def tile_list_clause_importability_scores_kernel(
             load_scale_rows(nc.scalar, tab_s, tab_scales, q)
         for q in range(4):
             load_scale_rows(nc.scalar if q < 2 else nc.gpsimd, w2s_raw, w2_scales, q)
+
         nc.gpsimd.dma_start(out=gain_t[:], in_=gain.rearrange("(b p t) -> p b t", b=NB, t=PACK))
-        nc.gpsimd.dma_start(out=dv_t[:], in_=dv.rearrange("(b p t) -> p b t", b=NB, t=PACK))
 
         f1 = [keep.tile([P, NP], F32, name="f1", tag="f1_%d" % s, align_bytes=64) for s in range(NSLICE)]
         for s in range(NSLICE):
@@ -123,6 +122,8 @@ def tile_list_clause_importability_scores_kernel(
         nc.vector.tensor_copy(v_s[:], tab_s[:].indirect(offs_t[:]))
         w2s_p = keep.tile([P, H], U8, name="w2s_p", tag="lane_c", align_bytes=64)
         deal_scales(w2s_p, w2s_raw)
+        dv_t = keep.tile([P, NB, PACK], F32, name="dv_t", tag="lane_d", align_bytes=64)
+        nc.sync.dma_start(out=dv_t[:], in_=dv.rearrange("(b p t) -> p b t", b=NB, t=PACK))
         v_w = [keep.tile([P, HALF], U32, name="v_w%d" % h, align_bytes=64) for h in range(2)]
         for h in range(2):
             nc.vector.tensor_copy(v_w[h][:], tab_w[:].bitcast(U32).indirect(offs_t[:, 32 * h : 32 * (h + 1)]))
@@ -157,10 +158,10 @@ def tile_list_clause_importability_scores_kernel(
 
         x1_op, x2_op, base_op = operand("x1"), operand("x2"), operand("base")
 
-        def weave(op, b, planes, c0, c1, slots=PACK):
+        def weave(op, b, planes, c0, c1, t0=0, t1=PACK):
             nc.scalar.activation(
-                out=op[0][b][:, c0:c1, 0:slots].rearrange("p (c i) t -> p c t i", i=4),
-                in_=planes[:, 0:slots, c0:c1].rearrange("p t (c i) -> p c t i", i=4),
+                out=op[0][b][:, c0:c1, t0:t1].rearrange("p (c i) t -> p c t i", i=4),
+                in_=planes[:, t0:t1, c0:c1].rearrange("p t (c i) -> p c t i", i=4),
                 func=ACT.Copy,
             )
 
@@ -182,8 +183,23 @@ def tile_list_clause_importability_scores_kernel(
                 in_=op[0][b][:, c0:c1, :].rearrange("p c t -> p (c t)"),
             )
 
-        def weave_base(b, planes, c0, c1):
-            weave(base_op, b, planes, c0, c1)
+        base_woven = {}
+
+        def weave_base(b, h, planes, tag):
+            base_woven[b, h] = keep.tile([P, 256, PACK], BF16, name="base_i", tag=tag, align_bytes=64)
+            nc.gpsimd.tensor_scalar(
+                base_woven[b, h][:], planes[:, :, 256 * h : 256 * (h + 1)].rearrange("p t c -> p c t"),
+                1.0, 0.0, ALU.mult, ALU.add,
+            )
+
+        def quantize_base(b):
+            for h in range(2):
+                cols = slice(256 * h, 256 * (h + 1))
+                nc.vector.quantize_mx(
+                    out=base_op[1][b][:, cols].bitcast(FP8X4),
+                    scales=base_op[2][b][:, cols],
+                    in_=base_woven[b, h][:].rearrange("p c t -> p (c t)"),
+                )
 
         x1_planes = [keep.tile([P, PACK, NP], F32, name="x1_pl%d" % b) for b in range(NB)]
         x2_planes = [keep.tile([P, PACK, NP], F32, name="x2_pl%d" % b) for b in range(NB)]
@@ -278,44 +294,42 @@ def tile_list_clause_importability_scores_kernel(
                 round_w1(staged["w1"], 1, 0, PACK, P // 2, P)
                 w1_c[1] = keep.tile([P, PASS], U32, name="w1_c1", tag="f1_1", align_bytes=64)
                 quantize_w1(1, 0, PACK)
-                staged["base0"] = load_rows(base_view[0])
-                staged["base1"] = load_base(1)
+                staged["base0"] = load_base(0)
+                staged["base1"] = load_rows(base_view[1])
             if s == 3:
-                place_woven(base_op, 1, "f1_2")
-                weave_base(1, staged["base1"], 0, 256)
-                weave_base(1, staged["base1"], 256, 512)
-                place_woven(base_op, 0, "base_i0")
-                weave_base(0, staged["base0"], 0, 256)
+                weave_base(0, 0, staged["base0"], "f1_2")
             if s == 4:
-                weave_base(0, staged["base0"], 256, 512)
-                place_codes(base_op, 0, "f1_3")
-                quantize(base_op, 0)
-                staged["rel"] = load_rows(rel.rearrange("(a p) j -> p a j", p=P))
+                weave_base(0, 1, staged["base0"], "f1_3")
                 weave(x2_op, 0, x2_planes[0], 0, 256)
+                weave(x1_op, 0, x1_planes[0], 0, 256)
             if s == 5:
+                weave_base(1, 0, staged["base1"], "f1_4")
                 weave(x2_op, 0, x2_planes[0], 256, 512)
                 place_codes(x2_op, 0, "x2_c0")
                 quantize(x2_op, 0)
-                weave(x1_op, 0, x1_planes[0], 0, 256)
-            if s == 6:
                 weave(x1_op, 0, x1_planes[0], 256, 512)
+            if s == 6:
+                place_codes(base_op, 0, "base_c0")
+                quantize_base(0)
+                weave_base(1, 1, staged["base1"], "f1_5")
+                staged["rel"] = load_rows(rel.rearrange("(a p) j -> p a j", p=P))
+        weave(x1_op, 1, x1_planes[1], 0, 512, 0, 2)
         pick(NSLICE - 2, bent)
         top = strongest(NSLICE - 1, r2_now)
         bent = bend(NSLICE - 1, top)
-        weave(x1_op, 1, x1_planes[1], 0, 512, 3)
         place_woven(x2_op, 1, "x2_i1")
-        weave(x2_op, 1, x2_planes[1], 0, 512, 3)
-        place_codes(base_op, 1, "f1_6")
-        quantize(base_op, 1)
-        pick(NSLICE - 1, bent)
-        place_codes(x1_op, 0, "f1_7")
+        weave(x2_op, 1, x2_planes[1], 0, 512, 0, 3)
+        place_codes(x1_op, 0, "f1_6")
         quantize(x1_op, 0)
+        pick(NSLICE - 1, bent)
+        place_codes(base_op, 1, "f1_7")
+        quantize_base(1)
         place_codes(x2_op, 1, "x2_c1")
         quantize(x2_op, 1)
         place_codes(x1_op, 1, "x1_c1")
         for a in range(MT):
             cols = slice(P * a, P * (a + 1))
-            nc.scalar.activation(out=x1_op[0][1][:, cols, 3], in_=x1_planes[1][:, 3, cols], func=ACT.Copy)
+            weave(x1_op, 1, x1_planes[1], cols.start, cols.stop, 2, PACK)
             quantize(x1_op, 1, cols.start, cols.stop)
 
         sums = [psum.tile([P, NP], F32, name="bank", tag="bank") for a in range(MT)]

from contextlib import ExitStack

import concourse.mybir as mybir

K, H, T, S, NP = 512, 1024, 4096, 1024, 512
FLOPS = 2 * (3 * K * H * S + 2 * H * NP * NP)

F32 = mybir.dt.float32
BF16 = mybir.dt.bfloat16
I32 = mybir.dt.int32
U32 = mybir.dt.uint32
U16 = mybir.dt.uint16
U8 = mybir.dt.uint8
FP8X4 = mybir.dt.float8_e4m3fn_x4
FP4X4 = mybir.dt.float4_e2m1fn_x4
ACT = mybir.ActivationFunctionType
ALU = mybir.AluOpType

P = 128
PACK = 4
PASS = P * PACK
HALF = 512
NB = H // PASS
NSLICE = NB * PACK
MT = NP // P


def tile_list_clause_importability_scores_kernel(
    tc, tab_words, tab_scales, w1, w2_words, w2_scales, w3_words, w3_scales,
    gain, dv, base, rel, offs, pos1, pos2, out,
):
    nc = tc.nc
    with ExitStack() as ctx:
        keep = ctx.enter_context(tc.tile_pool(name="keep", bufs=1))
        after_tab = ctx.enter_context(tc.tile_pool(name="after_tab", bufs=1))
        after_w2 = ctx.enter_context(tc.tile_pool(name="after_w2", bufs=1))
        work = ctx.enter_context(tc.tile_pool(name="work", bufs=2))
        psum = ctx.enter_context(tc.psum_pool(name="psum", bufs=8))

        offs_t = keep.tile([P, S // 16], U16, name="offs_t")
        pos1_t = keep.tile([P, NP // 16], U16, name="pos1_t")
        pos2_t = keep.tile([P, NP // 16], U16, name="pos2_t")
        tab_w = after_tab.tile([P, T], I32, name="tab_w", align_bytes=64, offset=0)
        tab_s = keep.tile([P, T], U8, name="tab_s", tag="lane_c", align_bytes=64)
        w2_raw = after_w2.tile([P, 2 * H], U8, name="w2_raw", align_bytes=64, offset=1536)
        w2s_raw = keep.tile([P, H], U8, name="w2s_raw", tag="lane_d", align_bytes=64)
        gain_t = keep.tile([P, NB, PACK], F32, name="gain_t")

        nc.vector.memset(tab_s[:].bitcast(I32), 0)
        nc.gpsimd.memset(w2s_raw[:].bitcast(I32), 0)

        def load_scale_rows(queue, tile, rows, quadrant):
            queue.dma_start(
                out=tile[:].bitcast(I32)[32 * quadrant : 32 * quadrant + 4, :],
                in_=rows[0, 4 * quadrant : 4 * quadrant + 4, :].bitcast(I32),
            )

        w3_view = w3_words[0].rearrange("p c i -> p (c i)").bitcast(I32)

        def load_w3(b):
            raw = after_w2.tile([P, PASS], I32, name="w3_raw", align_bytes=64, offset=0)
            nc.sync.dma_start(out=raw[:], in_=w3_view[:, PASS * b : PASS * (b + 1)])
            return raw

        def load_rows(rows):
            raw = after_w2.tile([P, PACK, 512], F32, name="raw", align_bytes=64, offset=3072)
            nc.sync.dma_start(out=raw[:], in_=rows)
            return raw

        def load_base(b):
            raw = after_tab.tile([P, PACK, NP], F32, name="base_raw", align_bytes=64, offset=8192)
            nc.sync.dma_start(out=raw[:], in_=base_view[b])
            return raw

        w1_view = w1.rearrange("(p j) r -> p j r", j=PACK)
        base_view = base.rearrange("(b p t) m -> b p t m", b=NB, t=PACK)

        nc.sync.dma_start(offs_t[:], offs)
        nc.sync.dma_start(pos1_t[:], pos1)
        nc.sync.dma_start(pos2_t[:], pos2)
        nc.sync.dma_start(out=w2_raw[:].bitcast(I32), in_=w2_words[0].bitcast(I32))
        nc.sync.dma_start(out=tab_w[:], in_=tab_words[0].rearrange("p t i -> p (t i)").bitcast(I32))
        for q in range(4):
            load_scale_rows(nc.scalar, tab_s, tab_scales, q)
        for q in range(4):
            load_scale_rows(nc.scalar if q < 2 else nc.gpsimd, w2s_raw, w2_scales, q)

        nc.gpsimd.dma_start(out=gain_t[:], in_=gain.rearrange("(b p t) -> p b t", b=NB, t=PACK))

        f1 = [keep.tile([P, NP], F32, name="f1", tag="f1_%d" % s, align_bytes=64) for s in range(NSLICE)]
        for s in range(NSLICE):
            b, t = divmod(s, PACK)
            nc.scalar.activation(out=f1[s][:], in_=gain_t[:, b, t : t + 1].to_broadcast([P, NP]), func=ACT.Copy)

        w2_p = keep.tile([P, 2 * H], U8, name="w2_p", align_bytes=64)
        w3_p = {}

        def deal_w3(raw, b, dealt):
            w3_p[b] = dealt
            nc.vector.tensor_copy(
                out=dealt[:].rearrange("p (t q) -> p q t", t=PACK),
                in_=raw[:].rearrange("p (q t) -> p q t", t=PACK),
            )

        def deal_scales(dealt, raw):
            nc.vector.tensor_copy(
                out=dealt[:].rearrange("p (b t q) -> p b t q", b=NB, t=PACK),
                in_=raw[:].rearrange("p (b q t) -> p b t q", b=NB, t=PACK),
            )

        nc.vector.tensor_copy(
            out=w2_p[:].rearrange("p (b t q e) -> p b t q e", b=NB, t=PACK, e=2),
            in_=w2_raw[:].rearrange("p (b q t e) -> p b t q e", b=NB, t=PACK, e=2),
        )
        w1_raw0 = load_rows(w1_view[:, :, 0:PASS])
        w3_raw0 = load_w3(0)
        w3s_raw = after_w2.tile([P, H], U8, name="w3s_raw", align_bytes=64, offset=2048)
        nc.gpsimd.memset(w3s_raw[:].bitcast(I32), 0)
        for q in range(4):
            load_scale_rows(nc.sync, w3s_raw, w3_scales, q)
        v_s = keep.tile([P, S], U8, name="v_s", align_bytes=64)
        nc.vector.tensor_copy(v_s[:], tab_s[:].indirect(offs_t[:]))
        w2s_p = keep.tile([P, H], U8, name="w2s_p", tag="lane_c", align_bytes=64)
        deal_scales(w2s_p, w2s_raw)
        dv_t = keep.tile([P, NB, PACK], F32, name="dv_t", tag="lane_d", align_bytes=64)
        nc.sync.dma_start(out=dv_t[:], in_=dv.rearrange("(b p t) -> p b t", b=NB, t=PACK))
        v_w = [keep.tile([P, HALF], U32, name="v_w%d" % h, align_bytes=64) for h in range(2)]
        for h in range(2):
            nc.vector.tensor_copy(v_w[h][:], tab_w[:].bitcast(U32).indirect(offs_t[:, 32 * h : 32 * (h + 1)]))

        w1_i = {
            (0, 0): keep.tile([P, 2, P, PACK], BF16, name="w1_i00", align_bytes=64),
            (0, 2): keep.tile([P, 2, P, PACK], BF16, name="w1_i02", align_bytes=64),
            (1, 0): keep.tile([P, PACK, P, PACK], BF16, name="w1_i10", align_bytes=64),
        }
        w1_c = {0: after_tab.tile([P, PASS], U32, name="w1_c0", align_bytes=64, offset=0)}
        w1_s = [keep.tile([P, PASS], U8, name="w1_s%d" % b, align_bytes=64) for b in range(NB)]

        def round_w1(raw, b, t0, t1, q0, q1):
            nc.scalar.activation(
                out=w1_i[b, t0][:].rearrange("p t q j -> p q t j")[:, q0:q1],
                in_=raw[:].rearrange("p j (q t) -> p q t j", t=PACK)[:, q0:q1, t0:t1, :],
                func=ACT.Copy,
            )

        def quantize_w1(b, t0, t1):
            nc.vector.quantize_mx(
                out=w1_c[b][:, P * t0 : P * t1].bitcast(FP8X4),
                scales=w1_s[b][:, P * t0 : P * t1],
                in_=w1_i[b, t0][:].rearrange("p t q j -> p (t q j)"),
            )

        def operand(name):
            woven = {}
            codes = {}
            scales = [keep.tile([P, NP], U8, name="%s_s%d" % (name, b), align_bytes=64) for b in range(NB)]
            return woven, codes, scales

        x1_op, x2_op, base_op = operand("x1"), operand("x2"), operand("base")

        def weave(op, b, planes, c0, c1, t0=0, t1=PACK):
            nc.scalar.activation(
                out=op[0][b][:, c0:c1, t0:t1].rearrange("p (c i) t -> p c t i", i=4),
                in_=planes[:, t0:t1, c0:c1].rearrange("p t (c i) -> p c t i", i=4),
                func=ACT.Copy,
            )

        def place_woven(op, b, tag):
            op[0][b] = keep.tile([P, NP, PACK], BF16, name="woven", tag=tag, align_bytes=64)

        for b in range(NB):
            place_woven(x1_op, b, "x1_i%d" % b)

        place_woven(x2_op, 0, "x2_i0")

        def place_codes(op, b, tag):
            op[1][b] = keep.tile([P, NP], U32, name="codes", tag=tag, align_bytes=64)

        def quantize(op, b, c0=0, c1=NP):
            nc.vector.quantize_mx(
                out=op[1][b][:, c0:c1].bitcast(FP8X4),
                scales=op[2][b][:, c0:c1],
                in_=op[0][b][:, c0:c1, :].rearrange("p c t -> p (c t)"),
            )

        base_woven = {}

        def weave_base(b, h, planes, tag):
            base_woven[b, h] = keep.tile([P, 256, PACK], BF16, name="base_i", tag=tag, align_bytes=64)
            nc.gpsimd.tensor_scalar(
                base_woven[b, h][:], planes[:, :, 256 * h : 256 * (h + 1)].rearrange("p t c -> p c t"),
                1.0, 0.0, ALU.mult, ALU.add,
            )

        def quantize_base(b):
            for h in range(2):
                cols = slice(256 * h, 256 * (h + 1))
                nc.vector.quantize_mx(
                    out=base_op[1][b][:, cols].bitcast(FP8X4),
                    scales=base_op[2][b][:, cols],
                    in_=base_woven[b, h][:].rearrange("p c t -> p (c t)"),
                )

        x1_planes = [keep.tile([P, PACK, NP], F32, name="x1_pl%d" % b) for b in range(NB)]
        x2_planes = [keep.tile([P, PACK, NP], F32, name="x2_pl%d" % b) for b in range(NB)]

        def product(codes, scales):
            banks = []
            for h in range(2):
                bank = psum.tile([P, HALF], F32, name="bank", tag="bank")
                nc.tensor.matmul_mx(
                    out=bank[:], lhsT=codes, lhsT_scale=scales,
                    rhs=v_w[h][:].bitcast(FP8X4), rhs_scale=v_s[:, HALF * h : HALF * (h + 1)],
                    start=True, stop=True,
                )
                banks.append(bank)
            return banks

        def second_reading(s):
            banks = product(w2_p[:, 2 * P * s : 2 * P * (s + 1)].bitcast(FP4X4), w2s_p[:, P * s : P * (s + 1)])
            if s == 0:
                r2 = [after_w2.tile([P, HALF], F32, name="r2_first%d" % h, align_bytes=64, offset=3072 + 2048 * h) for h in range(2)]
            else:
                r2 = [work.tile([P, HALF], F32, name="r2_%d" % h, bufs=3) for h in range(2)]
            for h in range(2):
                nc.scalar.activation(out=r2[h][:], in_=banks[h][:], func=ACT.Copy)
            return r2

        def strongest(s, r2):
            b, t = divmod(s, PACK)
            in_pass = slice(P * t, P * (t + 1))
            r1 = product(w1_c[b][:, in_pass].bitcast(FP8X4), w1_s[b][:, in_pass])
            r3 = product(w3_p[b][:, in_pass].bitcast(FP8X4), w3s_p[:, P * s : P * (s + 1)])
            last = s == NSLICE - 1
            pb, pt = divmod(s if last else (s - 1) % NSLICE, PACK)
            tag = "f1_%d" % (s - 1) if last else "turn_%d" % (s % 2)
            m12 = [keep.tile([P, HALF], F32, name="m12", tag=tag, align_bytes=64)[:], x1_planes[pb][:, pt, :]]
            if last:
                top = keep.tile([P, S], F32, name="top_last", tag="x2_i1", align_bytes=64)
            else:
                top = work.tile([P, S], F32, name="top")
            for h in range(2):
                nc.vector.tensor_tensor(m12[h], r1[h][:], r2[h][:], ALU.max)
            for h in range(2):
                nc.vector.tensor_tensor(top[:, HALF * h : HALF * (h + 1)], r3[h][:], m12[h], ALU.max)
            return top

        def bend(s, top):
            bent = work.tile([P, S], F32, name="bent", bufs=3)
            if s == NSLICE - 1:
                for h in range(2):
                    part = slice(HALF * h, HALF * (h + 1))
                    nc.scalar.activation(out=bent[:, part], in_=top[:, part], func=ACT.Tanh)
            else:
                nc.scalar.activation(out=bent[:], in_=top[:], func=ACT.Tanh)
            return bent

        def pick(s, bent):
            b, t = divmod(s, PACK)
            g2 = keep.tile([P, NP], F32, name="g2", tag="turn_%d" % ((s + 1) % 2), align_bytes=64)
            a2 = work.tile([P, NP], F32, name="a2")
            nc.vector.tensor_copy(g2[:], bent[:].indirect(pos2_t[:]))
            nc.vector.tensor_tensor(x1_planes[b][:, t, :], bent[:].indirect(pos1_t[:]), f1[s][:], ALU.mult)
            nc.scalar.activation(out=a2[:], in_=g2[:], func=ACT.Abs, scale=gain_t[:, b, t : t + 1])
            if s == NSLICE - 1:
                nc.scalar.activation(out=x2_op[0][b][:, :, t], in_=a2[:], func=ACT.Copy, scale=dv_t[:, b, t : t + 1])
            else:
                nc.gpsimd.tensor_scalar(x2_planes[b][:, t, :], a2[:], dv_t[:, b, t : t + 1], 0.0, ALU.mult, ALU.add)

        round_w1(w1_raw0, 0, 0, 2, 0, P)
        round_w1(w1_raw0, 0, 2, PACK, 0, P)
        r2_now = second_reading(0)
        quantize_w1(0, 0, 2)
        deal_w3(w3_raw0, 0, after_tab.tile([P, PASS], I32, name="w3_p0", align_bytes=64, offset=2048))
        w3s_p = after_tab.tile([P, H], U8, name="w3s_p", align_bytes=64, offset=4096)
        deal_scales(w3s_p, w3s_raw)
        quantize_w1(0, 2, PACK)
        top = strongest(0, r2_now)
        r2_now = second_reading(1)
        bent = bend(0, top)
        w3_raw1 = load_w3(1)
        staged = {}
        for s in range(1, NSLICE - 1):
            top = strongest(s, r2_now)
            r2_now = second_reading(s + 1)
            nxt = bend(s, top)
            pick(s - 1, bent)
            bent = nxt
            if s == 1:
                deal_w3(w3_raw1, 1, keep.tile([P, PASS], I32, name="w3_p1", tag="f1_0", align_bytes=64))
                staged["w1"] = load_rows(w1_view[:, :, PASS : 2 * PASS])
                round_w1(staged["w1"], 1, 0, PACK, 0, P // 2)
            if s == 2:
                round_w1(staged["w1"], 1, 0, PACK, P // 2, P)
                w1_c[1] = keep.tile([P, PASS], U32, name="w1_c1", tag="f1_1", align_bytes=64)
                quantize_w1(1, 0, PACK)
                staged["base0"] = load_base(0)
                staged["base1"] = load_rows(base_view[1])
            if s == 3:
                weave_base(0, 0, staged["base0"], "f1_2")
            if s == 4:
                weave_base(0, 1, staged["base0"], "f1_3")
                weave(x2_op, 0, x2_planes[0], 0, 256)
                weave(x1_op, 0, x1_planes[0], 0, 256)
            if s == 5:
                weave_base(1, 0, staged["base1"], "f1_4")
                weave(x2_op, 0, x2_planes[0], 256, 512)
                place_codes(x2_op, 0, "x2_c0")
                quantize(x2_op, 0)
                weave(x1_op, 0, x1_planes[0], 256, 512)
            if s == 6:
                place_codes(base_op, 0, "base_c0")
                quantize_base(0)
                weave_base(1, 1, staged["base1"], "f1_5")
                staged["rel"] = load_rows(rel.rearrange("(a p) j -> p a j", p=P))
        weave(x1_op, 1, x1_planes[1], 0, 512, 0, 2)
        pick(NSLICE - 2, bent)
        top = strongest(NSLICE - 1, r2_now)
        bent = bend(NSLICE - 1, top)
        place_woven(x2_op, 1, "x2_i1")
        weave(x2_op, 1, x2_planes[1], 0, 512, 0, 3)
        place_codes(x1_op, 0, "f1_6")
        quantize(x1_op, 0)
        pick(NSLICE - 1, bent)
        place_codes(base_op, 1, "f1_7")
        quantize_base(1)
        place_codes(x2_op, 1, "x2_c1")
        quantize(x2_op, 1)
        place_codes(x1_op, 1, "x1_c1")
        for a in range(MT):
            cols = slice(P * a, P * (a + 1))
            weave(x1_op, 1, x1_planes[1], cols.start, cols.stop, 2, PACK)
            quantize(x1_op, 1, cols.start, cols.stop)

        sums = [psum.tile([P, NP], F32, name="bank", tag="bank") for a in range(MT)]
        passes = ((base_op, 0), (x1_op, 0), (base_op, 1), (x1_op, 1))
        for first, last in ((0, 1), (1, 2), (2, 4)):
            for a in range(MT):
                cols = slice(P * a, P * (a + 1))
                for n in range(first, last):
                    op, b = passes[n]
                    nc.tensor.matmul_mx(
                        out=sums[a][:], lhsT=op[1][b][:, cols].bitcast(FP8X4), lhsT_scale=op[2][b][:, cols],
                        rhs=x2_op[1][b][:].bitcast(FP8X4), rhs_scale=x2_op[2][b][:],
                        start=(n == 0), stop=(n == len(passes) - 1),
                    )
        for a in range(MT):
            res = work.tile([P, NP], F32, name="res", bufs=4)
            nc.vector.tensor_tensor(res[:], sums[a][:], staged["rel"][:, a, :], ALU.mult)
            nc.sync.dma_start(out=out[P * a : P * (a + 1), :], in_=res[:])
